import numpy as np, ml_dtypes
CORES = [8,136,40,168]
N = 4
import mx_ref
NC, G, MB = 128, 2, 3
C = np.float32(0.047)
BF = ml_dtypes.bfloat16
def cut(t, i, w=512):
    return t[:, w * i:w * i + w]
def tile(rs):
    return np.stack(rs, axis=2).reshape(128, -1).astype(BF)
def layer(w, X):
    out = []
    for i in range(G):
        for t in range(len(X)):
            p = mx_ref.matmul(mx_ref.quantize(cut(w, len(X) * i + t)), X[t])
            z = p if t == 0 else z + p
        out.append(z)
    return out
def act(Z):
    return [np.maximum(s * z, 0) * C for z in Z for s in (1, -1)]
def setup_inputs(rng):
    def f(*shape):
        return mx_ref.flush((rng.standard_normal(shape, dtype=np.float32) * np.exp2(rng.integers(-2, 3, shape[:-1] + (1,)))).astype(BF))
    return {"x": f(N, 128, 4 * NC), "w1": f(N, 128, G * 512), "w2": f(N, 128, 512), "px": f(N, 128, MB * 4 * NC), "pw": f(N, 128, G * 512)}
def setup_inputs_blocks(rng):
    d = setup_inputs(rng)
    for k in ("x", "w1", "w2", "px"): d[k] = mx_ref.spread(d[k], rng, 4)
    for k in ("pw",): d[k] = mx_ref.spread(d[k], rng, 1)
    return d
def setup_inputs_wide(rng):
    d = setup_inputs(rng)
    for k in ("x", "w1", "w2", "px"): d[k] = mx_ref.flush((d[k].astype(np.float32) * np.exp2(rng.integers(-6, 7, (N, 1, 1))).astype(np.float32)).astype(BF))
    return d
def setup_inputs_zeros(rng):
    d = setup_inputs(rng); v = d["x"].reshape(N, 128, -1, 4).copy()
    v[np.broadcast_to((rng.random((N, 1, v.shape[2], 1)) < 0.33), v.shape)] = 0
    d["x"] = v.reshape(d["x"].shape)
    return d
def reference(x, w1, w2, px, pw):
    H = [mx_ref.quantize(tile(act(layer(w1[j], [mx_ref.quantize(x[j])])))) for j in range(N)]
    y = np.zeros((N, 128, N * NC), np.float32)
    for r in range(N):
        qw = mx_ref.quantize(w2[r])
        for j in range(N):
            y[r][:, NC * j:NC * j + NC] = mx_ref.matmul(qw, H[j])
    z = np.full((N, 128, MB * G * NC), np.nan, np.float32)
    for m in range(MB):
        a = mx_ref.quantize(cut(px[N - 1], m, 4 * NC))
        for s in range(N - 1):
            a = mx_ref.quantize(tile(act(layer(pw[s], [a]))))
        Z = layer(pw[N - 1], [a])
        for i in range(G):
            z[N - 1][:, NC * (G * m + i):NC * (G * m + i) + NC] = Z[i]
    return {"y": y, "z": z}

@@ -1,0 +1,225 @@
+from concourse.bass import DstId, RemoteDMATransfer
+from concourse.mybir import dt, AluOpType, ActivationFunctionType
+
+N, NC, G, MB = 4, 128, 2, 3
+C = 0.047
+CH = 2
+CW = MB * NC // CH
+F8, U8, BF, F32 = "float8_e4m3fn_x4", "uint8", "bfloat16", "float32"
+
+SCRATCH = {
+    "tx": ("sbuf", [128, 4 * NC], BF), "tw1": ("sbuf", [128, G * 512], BF), "tw2": ("sbuf", [128, 512], BF),
+    "tpx": ("sbuf", [128, MB * 4 * NC], BF), "tpw": ("sbuf", [128, G * 512], BF),
+    "th": ("sbuf", [128, 4 * NC], BF), "ta": ("sbuf", [128, MB * 4 * NC], BF), "tb": ("sbuf", [128, MB * 4 * NC], BF),
+    "xq": ("sbuf", [128, NC], F8), "xs": ("sbuf", [128, NC], U8),
+    "w1q": ("sbuf", [128, G * 128], F8), "w1s": ("sbuf", [128, G * 128], U8),
+    "w2q": ("sbuf", [128, 128], F8), "w2s": ("sbuf", [128, 128], U8),
+    "pwq": ("sbuf", [128, G * 128], F8), "pws": ("sbuf", [128, G * 128], U8),
+    "pvq": ("sbuf", [128, G * 128], F8), "pvs": ("sbuf", [128, G * 128], U8),
+    "hq": ("sbuf", [128, N * NC], F8), "hs": ("sbuf", [128, N * NC], U8),
+    "c0q": ("sbuf", [128, MB * NC], F8), "c0s": ("sbuf", [128, MB * NC], U8),
+    "c1q": ("sbuf", [128, MB * NC], F8), "c1s": ("sbuf", [128, MB * NC], U8),
+    "c2q": ("sbuf", [128, MB * NC], F8), "c2s": ("sbuf", [128, MB * NC], U8),
+    "c3q": ("sbuf", [128, MB * NC], F8), "c3s": ("sbuf", [128, MB * NC], U8),
+    "ysb": ("sbuf", [128, N * NC], F32), "zsb": ("sbuf", [128, MB * G * NC], F32),
+    "ps": ("psum", [128, 8 * 512], F32),
+}
+_TAGS = ["h", "k0", "k1", "m", "n"]
+SEMAPHORES = (["l_x", "l_w1", "l_w2", "l_pw", "l_px0", "l_px1", "q_x", "q_w1", "q_w2", "q_pw", "q_px0", "q_px1",
+               "in_px0", "in_px1", "in_w", "in_a1", "in_h", "in_a3_0", "in_a3_1", "sent",
+               "y0", "y1", "yc0", "yc1", "yst", "zz0_0", "zz0_1", "zz1_0", "zz1_1", "zc0_0", "zc0_1", "zc1_0", "zc1_1", "zst"]
+              + [p + t for t in _TAGS for p in ("z0", "z1", "ra", "rb", "qq")])
+
+
+def rank_program(g, core, T, topo):
+    rank = T.rank_of(core)
+    if rank is None:
+        return
+    S, cores, last = T.sem, T.cores, N - 1
+    ve, te, sc, sy = g.vector, g.tensor, g.scalar, g.sync
+    sent = [0]
+
+    def b8(ap):
+        return ap.bitcast(dt.uint8)
+
+    def count(mask):
+        return bin(mask).count("1")
+
+    ENG = count(topo.mask(core, cores[(rank + 1) % N]))
+
+    def send(out, in_, sem, to):
+        dst = cores[to]
+        rid, pid = topo.addr(dst, core)
+        mask = topo.mask(core, dst)
+        g.remote_dma(out_ap=out, in_ap=in_, remote_sem=S[sem], local_sem=S["sent"], pid=pid, routing_id=rid, dma_engine_mask=mask)
+        sent[0] += count(mask)
+
+    def send_pair(name, a, b, sem, to, dname=None):
+        d = dname or name
+        send(b8(T[d + "q"][:, a:b]), b8(T[name + "q"][:, a:b]), sem, to)
+        send(T[d + "s"][:, a:b], T[name + "s"][:, a:b], sem, to)
+
+    def spread(out, in_, sem):
+        ids, mask = [], topo.mask(core, cores[(rank + 1) % N])
+        for d in range(1, N):
+            dst = cores[(rank + d) % N]
+            rid, pid = topo.addr(dst, core)
+            ids.append(DstId(rid=rid, pnc=pid))
+            mask &= topo.mask(core, dst)
+        g.remote_dma_fused([RemoteDMATransfer(dst_ids=ids, dma_engine_mask=mask, remote_sem=S[sem], srcs=[in_],
+                                              dsts=[out] * len(ids))], local_sem=S["sent"])
+        sent[0] += count(mask)
+
+    def load(q, name, a=None, b=None, sem=None):
+        src, dst = T[name], T["t" + name]
+        if a is None:
+            a, b = 0, src.shape[1]
+        q.dma_start(dst[:, a:b], src[:, a:b]).then_inc(S[sem or "l_" + name], 16)
+
+    def quant(name):
+        n = T[name + "q"].shape[1]
+        ve.wait_ge(S["l_" + name], 16)
+        ve.quantize_mx(T[name + "q"][:, 0:n], T[name + "s"][:, 0:n], T["t" + name][:, 0:4 * n]).then_inc(S["q_" + name], 1)
+
+    def product(bank, w, i, c, a, b, sem):
+        te.matmul_mx(T.ps[:, 512 * bank:512 * bank + b - a], T[w + "q"][:, 128 * i:128 * i + 128], T[w + "s"][:, 128 * i:128 * i + 128],
+                     T[c + "q"][:, a:b], T[c + "s"][:, a:b], True, True).then_inc(S[sem], 1)
+
+    def step(tag, bank, w, c, a, b, tile, ob, o, oa, waits):
+        n = b - a
+        for sem, val in waits:
+            te.wait_ge(S[sem], val)
+        for i in range(G):
+            product(bank + i, w, i, c, a, b, "z%d%s" % (i, tag))
+        t, oe = T[tile], ob + 4 * n
+        z0, z1 = [T.ps[:, 512 * (bank + i):512 * (bank + i) + n] for i in range(G)]
+        sc.wait_ge(S["z0" + tag], 1)
+        for j, s in ((0, C), (1, -C)):
+            sc.activation(t[:, ob + j:oe:4], z0, ActivationFunctionType.Relu, scale=s).then_inc(S["ra" + tag], 1)
+        ve.wait_ge(S["z1" + tag], 1)
+        for j, s in ((2, C), (3, -C)):
+            ve.tensor_scalar(t[:, ob + j:oe:4], z1, s, 0.0, AluOpType.mult, AluOpType.max).then_inc(S["rb" + tag], 1)
+        ve.wait_ge(S["ra" + tag], 2)
+        ve.wait_ge(S["rb" + tag], 2)
+        ve.quantize_mx(T[o + "q"][:, oa:oa + n], T[o + "s"][:, oa:oa + n], t[:, ob:oe]).then_inc(S["qq" + tag], 1)
+
+    def chunk(k):
+        return CW * k, CW * k + CW
+
+    def make_h():
+        quant("x")
+        quant("w1")
+        step("h", 0, "w1", "x", 0, NC, "th", 0, "h", NC * rank, [("q_x", 1), ("q_w1", 1)])
+
+    def send_h():
+        a, b = NC * rank, NC * rank + NC
+        g.wait_ge(S["qqh"], 1)
+        spread(b8(T.hq[:, a:b]), b8(T.hq[:, a:b]), "in_h")
+        spread(T.hs[:, a:b], T.hs[:, a:b], "in_h")
+
+    def make_y():
+        te.wait_ge(S["q_w2"], 1)
+        te.wait_ge(S["qqh"], 1)
+        te.wait_ge(S["in_h"], 2 * ENG * (N - 1))
+        half = N * NC // 2
+        for i in range(2):
+            product(6 + i, "w2", 0, "h", half * i, half * i + half, "y%d" % i)
+        sc.wait_ge(S["y0"], 1)
+        sc.activation(T.ysb[:, 0:half], T.ps[:, 512 * 6:512 * 6 + half], ActivationFunctionType.Copy).then_inc(S["yc0"], 1)
+        ve.wait_ge(S["y1"], 1)
+        ve.tensor_copy(T.ysb[:, half:2 * half], T.ps[:, 512 * 7:512 * 7 + half]).then_inc(S["yc1"], 1)
+        sy.wait_ge(S["yc0"], 1)
+        sy.wait_ge(S["yc1"], 1)
+        sy.dma_start(T.y[:, 0:N * NC], T.ysb[:, 0:N * NC]).then_inc(S["yst"], 16)
+
+    if rank == last:
+        for k in range(CH):
+            load(sy, "px", 4 * CW * k, 4 * CW * k + 4 * CW, "l_px%d" % k)
+        load(sy, "x")
+        sc.wait_ge(S["l_px0"], 16)
+        for name in ("w1", "w2", "pw"):
+            load(sc, name)
+        for k in range(CH):
+            a, b = chunk(k)
+            ve.wait_ge(S["l_px%d" % k], 16)
+            ve.quantize_mx(T.c0q[:, a:b], T.c0s[:, a:b], T.tpx[:, 4 * a:4 * b]).then_inc(S["q_px%d" % k], 1)
+        g.wait_ge(S["q_px0"], 1)
+        send(b8(T.c0q[:, 0:CW]), b8(T.c0q[:, 0:CW]), "in_px0", 0)
+        g.wait_ge(S["q_px1"], 1)
+        send(T.c0s[:, 0:CH * CW], T.c0s[:, 0:CH * CW], "in_px0", 0)
+        send(b8(T.c0q[:, CW:CH * CW]), b8(T.c0q[:, CW:CH * CW]), "in_px1", 0)
+        make_h()
+        send_h()
+        quant("w2")
+        quant("pw")
+        make_y()
+        te.wait_ge(S["q_pw"], 1)
+        done = 0
+        for k in range(CH):
+            a, b = chunk(k)
+            te.wait_ge(S["in_a3_%d" % k], 2 * ENG)
+            for i in range(G):
+                product(2 + 2 * k + i, "pw", i, "c3", a, b, "zz%d_%d" % (k, i))
+            n = [0, 0]
+            for i in range(G):
+                q = (sc, ve)[i]
+                q.wait_ge(S["zz%d_%d" % (k, i)], 1)
+                c = a
+                while c < b:
+                    m, e = c // NC, min(b, c // NC * NC + NC)
+                    out = T.zsb[:, NC * (G * m + i) + c - NC * m:NC * (G * m + i) + e - NC * m]
+                    p = 512 * (2 + 2 * k + i) - a
+                    if i == 0:
+                        r = sc.activation(out, T.ps[:, p + c:p + e], ActivationFunctionType.Copy)
+                    else:
+                        r = ve.tensor_copy(out, T.ps[:, p + c:p + e])
+                    r.then_inc(S["zc%d_%d" % (k, i)], 1)
+                    n[i] += 1
+                    c = e
+            for i in range(G):
+                sy.wait_ge(S["zc%d_%d" % (k, i)], n[i])
+            upto = b // NC * G * NC
+            sy.dma_start(T.z[:, done:upto], T.zsb[:, done:upto]).then_inc(S["zst"], 16)
+            done = upto
+        sy.wait_ge(S["zst"], 16 * CH)
+    elif rank == 0:
+        load(sy, "x")
+        load(sc, "w1")
+        load(sy, "pw")
+        load(sc, "w2")
+        make_h()
+        send_h()
+        quant("pw")
+        for k in range(CH):
+            a, b = chunk(k)
+            if k == 0:
+                waits = [("q_pw", 1), ("in_px0", 2 * ENG)]
+            else:
+                waits = [("in_px1", ENG)]
+            step("k%d" % k, 2 + 2 * k, "pw", "c0", a, b, "ta", 4 * a, "c1", a, waits)
+            g.wait_ge(S["qqk%d" % k], 1)
+            send_pair("c1", a, b, "in_a1", 1 + k)
+        quant("w2")
+        make_y()
+    else:
+        k = rank - 1
+        a, b = chunk(k)
+        load(sy, "pw")
+        load(sc, "x")
+        load(sy, "w1")
+        load(sc, "w2")
+        quant("pw")
+        g.wait_ge(S["q_pw"], 1)
+        send_pair("pw", 0, G * 128, "in_w", 2 if rank == 1 else 1, "pv")
+        make_h()
+        send_h()
+        quant("w2")
+        own, other = ("pw", [("q_pw", 1)]), ("pv", [("in_w", 2 * ENG)])
+        first, second = (own, other) if rank == 1 else (other, own)
+        step("m", 2, first[0], "c1", a, b, "ta", 4 * a, "c2", a, first[1] + [("in_a1", 2 * ENG)])
+        step("n", 4, second[0], "c2", a, b, "tb", 4 * a, "c3", a, second[1] + [("qqm", 1)])
+        g.wait_ge(S["qqn"], 1)
+        send_pair("c3", a, b, "in_a3_%d" % k, last)
+        make_y()
+    sy.wait_ge(S["yst"], 16)
+    g.wait_ge(S["sent"], sent[0])

@@ -3,31 +3,36 @@ from concourse.mybir import dt, AluOpType, ActivationFunctionType
 
 N, NC, G, MB = 4, 128, 2, 3
 C = 0.047
+COLS = MB * NC
 CH = 2
-CW = MB * NC // CH
+CW = COLS // CH
+PIECES = [(NC * k, NC * k + NC) for k in range(MB)]
+RUNS = [[(0, 0, NC)], [(0, NC, CW)], [(1, CW, COLS)]]
 F8, U8, BF, F32 = "float8_e4m3fn_x4", "uint8", "bfloat16", "float32"
 
 SCRATCH = {
     "tx": ("sbuf", [128, 4 * NC], BF), "tw1": ("sbuf", [128, G * 512], BF), "tw2": ("sbuf", [128, 512], BF),
-    "tpx": ("sbuf", [128, MB * 4 * NC], BF), "tpw": ("sbuf", [128, G * 512], BF),
-    "th": ("sbuf", [128, 4 * NC], BF), "ta": ("sbuf", [128, MB * 4 * NC], BF), "tb": ("sbuf", [128, MB * 4 * NC], BF),
+    "tpx": ("sbuf", [128, 4 * COLS], BF), "tpw": ("sbuf", [128, G * 512], BF),
+    "th": ("sbuf", [128, 4 * NC], BF), "ta": ("sbuf", [128, 4 * COLS], BF), "tb": ("sbuf", [128, 4 * COLS], BF),
     "xq": ("sbuf", [128, NC], F8), "xs": ("sbuf", [128, NC], U8),
     "w1q": ("sbuf", [128, G * 128], F8), "w1s": ("sbuf", [128, G * 128], U8),
     "w2q": ("sbuf", [128, 128], F8), "w2s": ("sbuf", [128, 128], U8),
     "pwq": ("sbuf", [128, G * 128], F8), "pws": ("sbuf", [128, G * 128], U8),
     "pvq": ("sbuf", [128, G * 128], F8), "pvs": ("sbuf", [128, G * 128], U8),
     "hq": ("sbuf", [128, N * NC], F8), "hs": ("sbuf", [128, N * NC], U8),
-    "c0q": ("sbuf", [128, MB * NC], F8), "c0s": ("sbuf", [128, MB * NC], U8),
-    "c1q": ("sbuf", [128, MB * NC], F8), "c1s": ("sbuf", [128, MB * NC], U8),
-    "c2q": ("sbuf", [128, MB * NC], F8), "c2s": ("sbuf", [128, MB * NC], U8),
-    "c3q": ("sbuf", [128, MB * NC], F8), "c3s": ("sbuf", [128, MB * NC], U8),
-    "ysb": ("sbuf", [128, N * NC], F32), "zsb": ("sbuf", [128, MB * G * NC], F32),
+    "c0q": ("sbuf", [128, COLS], F8), "c0s": ("sbuf", [128, COLS], U8),
+    "c1q": ("sbuf", [128, COLS], F8), "c1s": ("sbuf", [128, COLS], U8),
+    "c2q": ("sbuf", [128, COLS], F8), "c2s": ("sbuf", [128, COLS], U8),
+    "c3q": ("sbuf", [128, COLS], F8), "c3s": ("sbuf", [128, COLS], U8),
+    "ysb": ("sbuf", [128, N * NC], F32), "zsb": ("sbuf", [128, G * COLS], F32),
     "ps": ("psum", [128, 8 * 512], F32),
 }
-_TAGS = ["h", "k0", "k1", "m", "n"]
-SEMAPHORES = (["l_x", "l_w1", "l_w2", "l_pw", "l_px0", "l_px1", "q_x", "q_w1", "q_w2", "q_pw", "q_px0", "q_px1",
-               "in_px0", "in_px1", "in_w", "in_a1", "in_h", "in_a3_0", "in_a3_1", "sent",
-               "y0", "y1", "yc0", "yc1", "yst", "zz0_0", "zz0_1", "zz1_0", "zz1_1", "zc0_0", "zc0_1", "zc1_0", "zc1_1", "zst"]
+_TAGS = ["h", "m", "n"] + ["k%d" % k for k in range(MB)]
+SEMAPHORES = (["l_x", "l_w1", "l_w2", "l_pw", "q_x", "q_w1", "q_w2", "q_pw"]
+              + [s + "%d" % k for s in ("l_px", "q_px", "in_px") for k in range(MB)]
+              + ["in_h%d" % j for j in range(N)]
+              + ["in_pl", "in_w", "in_a1", "in_a3_0", "in_a3_1", "out", "sent",
+                 "y0", "y1", "yc0", "yc1", "yst", "zz0_0", "zz0_1", "zz1_0", "zz1_1", "zc0_0", "zc0_1", "zc1_0", "zc1_1", "zst"]
               + [p + t for t in _TAGS for p in ("z0", "z1", "ra", "rb", "qq")])
 
 
@@ -37,38 +42,44 @@ def rank_program(g, core, T, topo):
         return
     S, cores, last = T.sem, T.cores, N - 1
     ve, te, sc, sy = g.vector, g.tensor, g.scalar, g.sync
-    sent = [0]
+    left = {"out": 0, "sent": 0}
 
     def b8(ap):
         return ap.bitcast(dt.uint8)
 
-    def count(mask):
-        return bin(mask).count("1")
+    def engines(mask):
+        return [e for e in range(mask.bit_length()) if mask >> e & 1]
 
-    ENG = count(topo.mask(core, cores[(rank + 1) % N]))
+    ENG = len(engines(topo.mask(core, cores[(rank + 1) % N])))
+    HALF = ENG // 2
 
-    def send(out, in_, sem, to):
+    def send(out, in_, sem, to, local, half=None):
         dst = cores[to]
         rid, pid = topo.addr(dst, core)
-        mask = topo.mask(core, dst)
-        g.remote_dma(out_ap=out, in_ap=in_, remote_sem=S[sem], local_sem=S["sent"], pid=pid, routing_id=rid, dma_engine_mask=mask)
-        sent[0] += count(mask)
+        eng = engines(topo.mask(core, dst))
+        if half is not None:
+            eng = eng[half::2]
+        g.remote_dma(out_ap=out, in_ap=in_, remote_sem=S[sem], local_sem=S[local], pid=pid, routing_id=rid,
+                     dma_engine_mask=sum(1 << e for e in eng))
+        left[local] += len(eng)
 
-    def send_pair(name, a, b, sem, to, dname=None):
-        d = dname or name
-        send(b8(T[d + "q"][:, a:b]), b8(T[name + "q"][:, a:b]), sem, to)
-        send(T[d + "s"][:, a:b], T[name + "s"][:, a:b], sem, to)
+    def codes(name, a, b, sem, to, dname=None, local="sent", half=None):
+        send(b8(T[(dname or name) + "q"][:, a:b]), b8(T[name + "q"][:, a:b]), sem, to, local, half)
 
-    def spread(out, in_, sem):
-        ids, mask = [], topo.mask(core, cores[(rank + 1) % N])
-        for d in range(1, N):
-            dst = cores[(rank + d) % N]
-            rid, pid = topo.addr(dst, core)
+    def plane(name, a, b, sem, to, dname=None, local="sent", half=None):
+        send(T[(dname or name) + "s"][:, a:b], T[name + "s"][:, a:b], sem, to, local, half)
+
+    def spread_h(to):
+        a, b = NC * rank, NC * rank + NC
+        ids, mask = [], topo.mask(core, cores[to[0]])
+        for r in to:
+            rid, pid = topo.addr(cores[r], core)
             ids.append(DstId(rid=rid, pnc=pid))
-            mask &= topo.mask(core, dst)
-        g.remote_dma_fused([RemoteDMATransfer(dst_ids=ids, dma_engine_mask=mask, remote_sem=S[sem], srcs=[in_],
-                                              dsts=[out] * len(ids))], local_sem=S["sent"])
-        sent[0] += count(mask)
+            mask &= topo.mask(core, cores[r])
+        for ap in (b8(T.hq[:, a:b]), T.hs[:, a:b]):
+            g.remote_dma_fused([RemoteDMATransfer(dst_ids=ids, dma_engine_mask=mask, remote_sem=S["in_h%d" % rank], srcs=[ap],
+                                                  dsts=[ap] * len(ids))], local_sem=S["sent"])
+            left["sent"] += len(engines(mask))
 
     def load(q, name, a=None, b=None, sem=None):
         src, dst = T[name], T["t" + name]
@@ -111,45 +122,49 @@ def rank_program(g, core, T, topo):
         quant("w1")
         step("h", 0, "w1", "x", 0, NC, "th", 0, "h", NC * rank, [("q_x", 1), ("q_w1", 1)])
 
-    def send_h():
-        a, b = NC * rank, NC * rank + NC
-        g.wait_ge(S["qqh"], 1)
-        spread(b8(T.hq[:, a:b]), b8(T.hq[:, a:b]), "in_h")
-        spread(T.hs[:, a:b], T.hs[:, a:b], "in_h")
-
     def make_y():
         te.wait_ge(S["q_w2"], 1)
         te.wait_ge(S["qqh"], 1)
-        te.wait_ge(S["in_h"], 2 * ENG * (N - 1))
+        for j in range(N):
+            if j != rank:
+                te.wait_ge(S["in_h%d" % j], 2 * ENG)
         half = N * NC // 2
         for i in range(2):
-            product(6 + i, "w2", 0, "h", half * i, half * i + half, "y%d" % i)
+            product(i, "w2", 0, "h", half * i, half * i + half, "y%d" % i)
         sc.wait_ge(S["y0"], 1)
-        sc.activation(T.ysb[:, 0:half], T.ps[:, 512 * 6:512 * 6 + half], ActivationFunctionType.Copy).then_inc(S["yc0"], 1)
+        sc.activation(T.ysb[:, 0:half], T.ps[:, 0:half], ActivationFunctionType.Copy).then_inc(S["yc0"], 1)
         ve.wait_ge(S["y1"], 1)
-        ve.tensor_copy(T.ysb[:, half:2 * half], T.ps[:, 512 * 7:512 * 7 + half]).then_inc(S["yc1"], 1)
+        ve.tensor_copy(T.ysb[:, half:2 * half], T.ps[:, 512:512 + half]).then_inc(S["yc1"], 1)
         sy.wait_ge(S["yc0"], 1)
         sy.wait_ge(S["yc1"], 1)
+        if left["out"]:
+            sy.wait_ge(S["out"], left["out"])
         sy.dma_start(T.y[:, 0:N * NC], T.ysb[:, 0:N * NC]).then_inc(S["yst"], 16)
 
     if rank == last:
-        for k in range(CH):
-            load(sy, "px", 4 * CW * k, 4 * CW * k + 4 * CW, "l_px%d" % k)
+        for k, (a, b) in enumerate(PIECES):
+            load(sy, "px", 4 * a, 4 * b, "l_px%d" % k)
         load(sy, "x")
         sc.wait_ge(S["l_px0"], 16)
-        for name in ("w1", "w2", "pw"):
-            load(sc, name)
-        for k in range(CH):
-            a, b = chunk(k)
+        load(sc, "w1")
+        for k, (a, b) in enumerate(PIECES):
             ve.wait_ge(S["l_px%d" % k], 16)
             ve.quantize_mx(T.c0q[:, a:b], T.c0s[:, a:b], T.tpx[:, 4 * a:4 * b]).then_inc(S["q_px%d" % k], 1)
         g.wait_ge(S["q_px0"], 1)
-        send(b8(T.c0q[:, 0:CW]), b8(T.c0q[:, 0:CW]), "in_px0", 0)
-        g.wait_ge(S["q_px1"], 1)
-        send(T.c0s[:, 0:CH * CW], T.c0s[:, 0:CH * CW], "in_px0", 0)
-        send(b8(T.c0q[:, CW:CH * CW]), b8(T.c0q[:, CW:CH * CW]), "in_px1", 0)
+        for k, (a, b) in enumerate(PIECES):
+            codes("c0", a, b, "in_px%d" % k, 0, None, "out", None if k else 0)
+            if k == 0:
+                for i in range(1, MB):
+                    g.wait_ge(S["q_px%d" % i], 1)
+                plane("c0", 0, COLS, "in_pl", 0, None, "out", 1)
+        sy.wait_ge(S["out"], left["out"])
+        load(sy, "w2")
+        load(sy, "pw")
         make_h()
-        send_h()
+        g.wait_ge(S["qqh"], 1)
+        g.wait_ge(S["l_w2"], 16)
+        g.wait_ge(S["l_pw"], 16)
+        spread_h([0, 1, 2])
         quant("w2")
         quant("pw")
         make_y()
@@ -188,38 +203,53 @@ def rank_program(g, core, T, topo):
         load(sy, "pw")
         load(sc, "w2")
         make_h()
-        send_h()
+        g.wait_ge(S["qqh"], 1)
+        spread_h([last])
         quant("pw")
-        for k in range(CH):
-            a, b = chunk(k)
+        for k, (a, b) in enumerate(PIECES):
             if k == 0:
-                waits = [("q_pw", 1), ("in_px0", 2 * ENG)]
+                waits = [("q_pw", 1), ("in_px0", HALF), ("in_pl", HALF)]
             else:
-                waits = [("in_px1", ENG)]
+                waits = [("in_px%d" % k, ENG)]
             step("k%d" % k, 2 + 2 * k, "pw", "c0", a, b, "ta", 4 * a, "c1", a, waits)
             g.wait_ge(S["qqk%d" % k], 1)
-            send_pair("c1", a, b, "in_a1", 1 + k)
+            for i, c, e in RUNS[k]:
+                codes("c1", c, e, "in_a1", 1 + i)
+                if e == chunk(i)[1]:
+                    plane("c1", chunk(i)[0], e, "in_a1", 1 + i)
+        spread_h([1, 2])
         quant("w2")
         make_y()
     else:
         k = rank - 1
         a, b = chunk(k)
+        partner = 3 - rank
         load(sy, "pw")
         load(sc, "x")
         load(sy, "w1")
         load(sc, "w2")
         quant("pw")
         g.wait_ge(S["q_pw"], 1)
-        send_pair("pw", 0, G * 128, "in_w", 2 if rank == 1 else 1, "pv")
+        codes("pw", 0, G * 128, "in_w", partner, "pv")
+        plane("pw", 0, G * 128, "in_w", partner, "pv")
         make_h()
-        send_h()
+        g.wait_ge(S["qqh"], 1)
+        spread_h([partner])
+        spread_h([last])
         quant("w2")
         own, other = ("pw", [("q_pw", 1)]), ("pv", [("in_w", 2 * ENG)])
         first, second = (own, other) if rank == 1 else (other, own)
-        step("m", 2, first[0], "c1", a, b, "ta", 4 * a, "c2", a, first[1] + [("in_a1", 2 * ENG)])
+        writes = 1 + sum(1 for p in RUNS for run in p if run[0] == k)
+        here = ("in_a1", writes * ENG)
+        step("m", 2, first[0], "c1", a, b, "ta", 4 * a, "c2", a, first[1] + [here])
         step("n", 4, second[0], "c2", a, b, "tb", 4 * a, "c3", a, second[1] + [("qqm", 1)])
+        g.wait_ge(S[here[0]], here[1])
+        spread_h([0])
         g.wait_ge(S["qqn"], 1)
-        send_pair("c3", a, b, "in_a3_%d" % k, last)
+        codes("c3", a, b, "in_a3_%d" % k, last, None, "out")
+        plane("c3", a, b, "in_a3_%d" % k, last, None, "out")
         make_y()
     sy.wait_ge(S["yst"], 16)
-    g.wait_ge(S["sent"], sent[0])
+    for s in ("out", "sent"):
+        if left[s]:
+            g.wait_ge(S[s], left[s])

from concourse.bass import DstId, RemoteDMATransfer
from concourse.mybir import dt, AluOpType, ActivationFunctionType

N, NC, G, MB = 4, 128, 2, 3
C = 0.047
COLS = MB * NC
CH = 2
CW = COLS // CH
PIECES = [(NC * k, NC * k + NC) for k in range(MB)]
RUNS = [[(0, 0, NC)], [(0, NC, CW)], [(1, CW, COLS)]]
F8, U8, BF, F32 = "float8_e4m3fn_x4", "uint8", "bfloat16", "float32"

SCRATCH = {
    "tx": ("sbuf", [128, 4 * NC], BF), "tw1": ("sbuf", [128, G * 512], BF), "tw2": ("sbuf", [128, 512], BF),
    "tpx": ("sbuf", [128, 4 * COLS], BF), "tpw": ("sbuf", [128, G * 512], BF),
    "th": ("sbuf", [128, 4 * NC], BF), "ta": ("sbuf", [128, 4 * COLS], BF), "tb": ("sbuf", [128, 4 * COLS], BF),
    "xq": ("sbuf", [128, NC], F8), "xs": ("sbuf", [128, NC], U8),
    "w1q": ("sbuf", [128, G * 128], F8), "w1s": ("sbuf", [128, G * 128], U8),
    "w2q": ("sbuf", [128, 128], F8), "w2s": ("sbuf", [128, 128], U8),
    "pwq": ("sbuf", [128, G * 128], F8), "pws": ("sbuf", [128, G * 128], U8),
    "pvq": ("sbuf", [128, G * 128], F8), "pvs": ("sbuf", [128, G * 128], U8),
    "hq": ("sbuf", [128, N * NC], F8), "hs": ("sbuf", [128, N * NC], U8),
    "c0q": ("sbuf", [128, COLS], F8), "c0s": ("sbuf", [128, COLS], U8),
    "c1q": ("sbuf", [128, COLS], F8), "c1s": ("sbuf", [128, COLS], U8),
    "c2q": ("sbuf", [128, COLS], F8), "c2s": ("sbuf", [128, COLS], U8),
    "c3q": ("sbuf", [128, COLS], F8), "c3s": ("sbuf", [128, COLS], U8),
    "ysb": ("sbuf", [128, N * NC], F32), "zsb": ("sbuf", [128, G * COLS], F32),
    "ps": ("psum", [128, 8 * 512], F32),
}
_TAGS = ["h", "m", "n"] + ["k%d" % k for k in range(MB)]
SEMAPHORES = (["l_x", "l_w1", "l_w2", "l_pw", "q_x", "q_w1", "q_w2", "q_pw"]
              + [s + "%d" % k for s in ("l_px", "q_px", "in_px") for k in range(MB)]
              + ["in_h%d" % j for j in range(N)]
              + ["in_pl", "in_w", "in_a1", "in_a3_0", "in_a3_1", "out", "sent",
                 "y0", "y1", "yc0", "yc1", "yst", "zz0_0", "zz0_1", "zz1_0", "zz1_1", "zc0_0", "zc0_1", "zc1_0", "zc1_1", "zst"]
              + [p + t for t in _TAGS for p in ("z0", "z1", "ra", "rb", "qq")])


def rank_program(g, core, T, topo):
    rank = T.rank_of(core)
    if rank is None:
        return
    S, cores, last = T.sem, T.cores, N - 1
    ve, te, sc, sy = g.vector, g.tensor, g.scalar, g.sync
    left = {"out": 0, "sent": 0}

    def b8(ap):
        return ap.bitcast(dt.uint8)

    def engines(mask):
        return [e for e in range(mask.bit_length()) if mask >> e & 1]

    ENG = len(engines(topo.mask(core, cores[(rank + 1) % N])))
    HALF = ENG // 2

    def send(out, in_, sem, to, local, half=None):
        dst = cores[to]
        rid, pid = topo.addr(dst, core)
        eng = engines(topo.mask(core, dst))
        if half is not None:
            eng = eng[half::2]
        g.remote_dma(out_ap=out, in_ap=in_, remote_sem=S[sem], local_sem=S[local], pid=pid, routing_id=rid,
                     dma_engine_mask=sum(1 << e for e in eng))
        left[local] += len(eng)

    def codes(name, a, b, sem, to, dname=None, local="sent", half=None):
        send(b8(T[(dname or name) + "q"][:, a:b]), b8(T[name + "q"][:, a:b]), sem, to, local, half)

    def plane(name, a, b, sem, to, dname=None, local="sent", half=None):
        send(T[(dname or name) + "s"][:, a:b], T[name + "s"][:, a:b], sem, to, local, half)

    def spread_h(to):
        a, b = NC * rank, NC * rank + NC
        ids, mask = [], topo.mask(core, cores[to[0]])
        for r in to:
            rid, pid = topo.addr(cores[r], core)
            ids.append(DstId(rid=rid, pnc=pid))
            mask &= topo.mask(core, cores[r])
        for ap in (b8(T.hq[:, a:b]), T.hs[:, a:b]):
            g.remote_dma_fused([RemoteDMATransfer(dst_ids=ids, dma_engine_mask=mask, remote_sem=S["in_h%d" % rank], srcs=[ap],
                                                  dsts=[ap] * len(ids))], local_sem=S["sent"])
            left["sent"] += len(engines(mask))

    def load(q, name, a=None, b=None, sem=None):
        src, dst = T[name], T["t" + name]
        if a is None:
            a, b = 0, src.shape[1]
        q.dma_start(dst[:, a:b], src[:, a:b]).then_inc(S[sem or "l_" + name], 16)

    def quant(name):
        n = T[name + "q"].shape[1]
        ve.wait_ge(S["l_" + name], 16)
        ve.quantize_mx(T[name + "q"][:, 0:n], T[name + "s"][:, 0:n], T["t" + name][:, 0:4 * n]).then_inc(S["q_" + name], 1)

    def product(bank, w, i, c, a, b, sem):
        te.matmul_mx(T.ps[:, 512 * bank:512 * bank + b - a], T[w + "q"][:, 128 * i:128 * i + 128], T[w + "s"][:, 128 * i:128 * i + 128],
                     T[c + "q"][:, a:b], T[c + "s"][:, a:b], True, True).then_inc(S[sem], 1)

    def step(tag, bank, w, c, a, b, tile, ob, o, oa, waits):
        n = b - a
        for sem, val in waits:
            te.wait_ge(S[sem], val)
        for i in range(G):
            product(bank + i, w, i, c, a, b, "z%d%s" % (i, tag))
        t, oe = T[tile], ob + 4 * n
        z0, z1 = [T.ps[:, 512 * (bank + i):512 * (bank + i) + n] for i in range(G)]
        sc.wait_ge(S["z0" + tag], 1)
        for j, s in ((0, C), (1, -C)):
            sc.activation(t[:, ob + j:oe:4], z0, ActivationFunctionType.Relu, scale=s).then_inc(S["ra" + tag], 1)
        ve.wait_ge(S["z1" + tag], 1)
        for j, s in ((2, C), (3, -C)):
            ve.tensor_scalar(t[:, ob + j:oe:4], z1, s, 0.0, AluOpType.mult, AluOpType.max).then_inc(S["rb" + tag], 1)
        ve.wait_ge(S["ra" + tag], 2)
        ve.wait_ge(S["rb" + tag], 2)
        ve.quantize_mx(T[o + "q"][:, oa:oa + n], T[o + "s"][:, oa:oa + n], t[:, ob:oe]).then_inc(S["qq" + tag], 1)

    def chunk(k):
        return CW * k, CW * k + CW

    def make_h():
        quant("x")
        quant("w1")
        step("h", 0, "w1", "x", 0, NC, "th", 0, "h", NC * rank, [("q_x", 1), ("q_w1", 1)])

    def make_y():
        te.wait_ge(S["q_w2"], 1)
        te.wait_ge(S["qqh"], 1)
        for j in range(N):
            if j != rank:
                te.wait_ge(S["in_h%d" % j], 2 * ENG)
        half = N * NC // 2
        for i in range(2):
            product(i, "w2", 0, "h", half * i, half * i + half, "y%d" % i)
        sc.wait_ge(S["y0"], 1)
        sc.activation(T.ysb[:, 0:half], T.ps[:, 0:half], ActivationFunctionType.Copy).then_inc(S["yc0"], 1)
        ve.wait_ge(S["y1"], 1)
        ve.tensor_copy(T.ysb[:, half:2 * half], T.ps[:, 512:512 + half]).then_inc(S["yc1"], 1)
        sy.wait_ge(S["yc0"], 1)
        sy.wait_ge(S["yc1"], 1)
        if left["out"]:
            sy.wait_ge(S["out"], left["out"])
        sy.dma_start(T.y[:, 0:N * NC], T.ysb[:, 0:N * NC]).then_inc(S["yst"], 16)

    if rank == last:
        for k, (a, b) in enumerate(PIECES):
            load(sy, "px", 4 * a, 4 * b, "l_px%d" % k)
        load(sy, "x")
        sc.wait_ge(S["l_px0"], 16)
        load(sc, "w1")
        for k, (a, b) in enumerate(PIECES):
            ve.wait_ge(S["l_px%d" % k], 16)
            ve.quantize_mx(T.c0q[:, a:b], T.c0s[:, a:b], T.tpx[:, 4 * a:4 * b]).then_inc(S["q_px%d" % k], 1)
        g.wait_ge(S["q_px0"], 1)
        for k, (a, b) in enumerate(PIECES):
            codes("c0", a, b, "in_px%d" % k, 0, None, "out", None if k else 0)
            if k == 0:
                for i in range(1, MB):
                    g.wait_ge(S["q_px%d" % i], 1)
                plane("c0", 0, COLS, "in_pl", 0, None, "out", 1)
        sy.wait_ge(S["out"], left["out"])
        load(sy, "w2")
        load(sy, "pw")
        make_h()
        g.wait_ge(S["qqh"], 1)
        g.wait_ge(S["l_w2"], 16)
        g.wait_ge(S["l_pw"], 16)
        spread_h([0, 1, 2])
        quant("w2")
        quant("pw")
        make_y()
        te.wait_ge(S["q_pw"], 1)
        done = 0
        for k in range(CH):
            a, b = chunk(k)
            te.wait_ge(S["in_a3_%d" % k], 2 * ENG)
            for i in range(G):
                product(2 + 2 * k + i, "pw", i, "c3", a, b, "zz%d_%d" % (k, i))
            n = [0, 0]
            for i in range(G):
                q = (sc, ve)[i]
                q.wait_ge(S["zz%d_%d" % (k, i)], 1)
                c = a
                while c < b:
                    m, e = c // NC, min(b, c // NC * NC + NC)
                    out = T.zsb[:, NC * (G * m + i) + c - NC * m:NC * (G * m + i) + e - NC * m]
                    p = 512 * (2 + 2 * k + i) - a
                    if i == 0:
                        r = sc.activation(out, T.ps[:, p + c:p + e], ActivationFunctionType.Copy)
                    else:
                        r = ve.tensor_copy(out, T.ps[:, p + c:p + e])
                    r.then_inc(S["zc%d_%d" % (k, i)], 1)
                    n[i] += 1
                    c = e
            for i in range(G):
                sy.wait_ge(S["zc%d_%d" % (k, i)], n[i])
            upto = b // NC * G * NC
            sy.dma_start(T.z[:, done:upto], T.zsb[:, done:upto]).then_inc(S["zst"], 16)
            done = upto
        sy.wait_ge(S["zst"], 16 * CH)
    elif rank == 0:
        load(sy, "x")
        load(sc, "w1")
        load(sy, "pw")
        load(sc, "w2")
        make_h()
        g.wait_ge(S["qqh"], 1)
        spread_h([last])
        quant("pw")
        for k, (a, b) in enumerate(PIECES):
            if k == 0:
                waits = [("q_pw", 1), ("in_px0", HALF), ("in_pl", HALF)]
            else:
                waits = [("in_px%d" % k, ENG)]
            step("k%d" % k, 2 + 2 * k, "pw", "c0", a, b, "ta", 4 * a, "c1", a, waits)
            g.wait_ge(S["qqk%d" % k], 1)
            for i, c, e in RUNS[k]:
                codes("c1", c, e, "in_a1", 1 + i)
                if e == chunk(i)[1]:
                    plane("c1", chunk(i)[0], e, "in_a1", 1 + i)
        spread_h([1, 2])
        quant("w2")
        make_y()
    else:
        k = rank - 1
        a, b = chunk(k)
        partner = 3 - rank
        load(sy, "pw")
        load(sc, "x")
        load(sy, "w1")
        load(sc, "w2")
        quant("pw")
        g.wait_ge(S["q_pw"], 1)
        codes("pw", 0, G * 128, "in_w", partner, "pv")
        plane("pw", 0, G * 128, "in_w", partner, "pv")
        make_h()
        g.wait_ge(S["qqh"], 1)
        spread_h([partner])
        spread_h([last])
        quant("w2")
        own, other = ("pw", [("q_pw", 1)]), ("pv", [("in_w", 2 * ENG)])
        first, second = (own, other) if rank == 1 else (other, own)
        writes = 1 + sum(1 for p in RUNS for run in p if run[0] == k)
        here = ("in_a1", writes * ENG)
        step("m", 2, first[0], "c1", a, b, "ta", 4 * a, "c2", a, first[1] + [here])
        step("n", 4, second[0], "c2", a, b, "tb", 4 * a, "c3", a, second[1] + [("qqm", 1)])
        g.wait_ge(S[here[0]], here[1])
        spread_h([0])
        g.wait_ge(S["qqn"], 1)
        codes("c3", a, b, "in_a3_%d" % k, last, None, "out")
        plane("c3", a, b, "in_a3_%d" % k, last, None, "out")
        make_y()
    sy.wait_ge(S["yst"], 16)
    for s in ("out", "sent"):
        if left[s]:
            g.wait_ge(S[s], left[s])
